import numpy as np
import ml_dtypes


def mxq(x, axis, fmt="e4m3"):
    dtype, down = {"e4m3": (ml_dtypes.float8_e4m3fn, 7), "e5m2": (ml_dtypes.float8_e5m2, 14)}[fmt]
    v = np.moveaxis(np.asarray(x, np.float32).astype(ml_dtypes.bfloat16).astype(np.float64), axis, -1)
    blocks = v.reshape(v.shape[:-1] + (-1, 32))
    amax = np.abs(blocks).max(-1, keepdims=True)
    byte = np.maximum(np.where(amax > 0, np.frexp(amax)[1] - 1 + 127, 0) - down, 1)
    scale = np.exp2(byte - 127.0)
    codes = (blocks / scale).astype(np.float32).astype(dtype).astype(np.float64)
    return np.moveaxis((codes * scale).reshape(v.shape), -1, axis)


WIDE = False


def mx_kscale(k):
    if not WIDE:
        return np.ones(k)
    levels = np.array([30, -30])
    if k % 512:
        return np.exp2(np.random.permutation(np.resize(levels, k // 32))).repeat(32)
    a = np.empty((k // 512, 16))
    for p in range(k // 512):
        a[p, :8] = np.random.permutation(np.resize(levels, 8))
        for g in range(8):
            far = levels[np.abs(levels - a[p, g]) >= 10]
            a[p, g + 8] = far[np.random.randint(len(far))]
    return np.exp2(a.ravel()).repeat(32)


def f64(x):
    return np.asarray(x).astype(np.float64)


def striped(idx):
    return np.tile(np.asarray(idx).reshape(-1, 16).T, (8, 1)).astype(np.uint16)


def unstriped(offs):
    return offs[:16].T.reshape(-1).astype(np.int64)


E2M1 = np.array([0.0, 0.5, 1.0, 1.5, 2.0, 3.0, 4.0, 6.0, -0.0, -0.5, -1.0, -1.5, -2.0, -3.0, -4.0, -6.0])


def pack_weight(w, fmt):
    k, n = w.shape
    w = f64(np.asarray(w, np.float32).astype(ml_dtypes.bfloat16)).reshape(k // 32, 32, n)
    amax = np.abs(w).max(1)
    if fmt in ("e4m3", "e5m2"):
        byte = np.frexp(amax)[1] - 1 + 127 - (7 if fmt == "e4m3" else 14)
    else:
        mant, ex = np.frexp(amax / 6.0)
        byte = np.where(mant > 0.5, ex, ex - 1) + 127
    byte = np.clip(np.where(amax > 0, byte, 1), 1, 254)
    scaled = (w * np.exp2(127.0 - byte)[:, None, :]).reshape(k, n).astype(np.float32)
    by_word = np.ascontiguousarray(scaled.reshape(k // 512, 128, 4, n).transpose(0, 1, 3, 2))
    if fmt in ("e4m3", "e5m2"):
        words = by_word.astype(ml_dtypes.float8_e4m3fn if fmt == "e4m3" else ml_dtypes.float8_e5m2).view(np.uint8)
    else:
        c = by_word.astype(ml_dtypes.float4_e2m1fn).view(np.uint8) & 0xF
        words = (c[..., 0::2] | (c[..., 1::2] << 4)).reshape(k // 512, 128, 2 * n)
    return np.ascontiguousarray(words), np.ascontiguousarray(byte.astype(np.uint8).reshape(k // 512, 16, n))


def unpack_weight(words, scales, fmt):
    g, _, n = scales.shape
    words = np.ascontiguousarray(words).reshape(g, 128, n, -1)
    if fmt in ("e4m3", "e5m2"):
        vals = words.view(ml_dtypes.float8_e4m3fn if fmt == "e4m3" else ml_dtypes.float8_e5m2).astype(np.float64)
    else:
        nib = np.empty((g, 128, n, 4), np.uint8)
        nib[..., 0::2] = words & 0xF
        nib[..., 1::2] = words >> 4
        vals = E2M1[nib]
    vals = vals * np.repeat(np.exp2(scales.astype(np.float64) - 127.0), 8, axis=1)[..., None]
    return vals.transpose(0, 1, 3, 2).reshape(g * 512, n)


K, T, J, R, C, O, N, U = 512, 1024, 256, 512, 512, 256, 256, 128


def setup_inputs():
    n = np.random.standard_normal
    idx = np.random.permutation(T)[:J]
    idx2 = np.random.permutation(C)[:J]
    idx3 = np.random.permutation(C)[:O]
    idx4 = np.random.permutation(C)[:O]
    idx5 = np.random.permutation(T)[:O]
    idx6 = np.random.permutation(O)[:U]
    idx7 = np.random.permutation(O)[:U]
    fk = mx_kscale(K)
    fr = mx_kscale(R)
    xtp = pack_weight(n((K, T)) / fk[:, None], "e5m2")
    wp = pack_weight(n((K, R)) * 1 / np.sqrt(K) * fk[:, None] * fr, "e2m1")
    wbp = pack_weight(n((R, N)) * 1 / np.sqrt(R) / fr[:, None], "e2m1")
    wsp = pack_weight(n((K, N)) * 1 / np.sqrt(K) * fk[:, None], "e2m1")
    return {
        "xt_words": xtp[0],
        "xt_scales": xtp[1],
        "w_words": wp[0],
        "w_scales": wp[1],
        "sa": (np.random.uniform(0.5, 1.6, (R, 1))).astype(np.float32),
        "sb": (np.random.uniform(0.5, 1.6, (R, 1))).astype(np.float32),
        "wb_words": wbp[0],
        "wb_scales": wbp[1],
        "ws_words": wsp[0],
        "ws_scales": wsp[1],
        "so": (np.random.uniform(0.5, 1.6, (N, 1))).astype(np.float32),
        "offs": striped(idx),
        "offs2": striped(idx2),
        "offs3": striped(idx3),
        "offs4": striped(idx4),
        "offs5": striped(idx5),
        "offs6": striped(idx6),
        "offs7": striped(idx7),
    }


def reference(xt_words, xt_scales, w_words, w_scales, sa, sb, wb_words, wb_scales, ws_words, ws_scales, so, offs, offs2, offs3, offs4, offs5, offs6, offs7):
    idx = unstriped(offs)
    idx2 = unstriped(offs2)
    idx3 = unstriped(offs3)
    idx4 = unstriped(offs4)
    idx5 = unstriped(offs5)
    idx6 = unstriped(offs6)
    idx7 = unstriped(offs7)
    xtu = unpack_weight(xt_words, xt_scales, "e5m2")
    wu = unpack_weight(w_words, w_scales, "e2m1")
    wbu = unpack_weight(wb_words, wb_scales, "e2m1")
    wsu = unpack_weight(ws_words, ws_scales, "e2m1")
    xtidxg = xtu[:, idx]
    a = wu.T @ xtidxg
    pw = np.zeros((R, C))
    pw[:, idx2] = a
    hid = np.abs(pw[:, idx3] * f64(sa) - pw[:, idx4] * f64(sb))
    hidq = mxq(hid, 0, "e4m3")
    xtidx5g = xtu[:, idx5]
    p = wbu.T @ hidq + wsu.T @ xtidx5g
    y = p[:, idx6] - p[:, idx7] * f64(so)
    return y

@@ -1,0 +1,171 @@
+from contextlib import ExitStack
+
+import concourse.mybir as mybir
+
+K, T, J, R, C, O, N, U = 512, 1024, 256, 512, 512, 256, 256, 128
+FLOPS = 2 * K * R * J + 2 * R * N * O + 2 * K * N * O
+
+F32 = mybir.dt.float32
+BF16 = mybir.dt.bfloat16
+I32 = mybir.dt.int32
+U32 = mybir.dt.uint32
+U16 = mybir.dt.uint16
+U8 = mybir.dt.uint8
+E4M3 = mybir.dt.float8_e4m3fn_x4
+E5M2 = mybir.dt.float8_e5m2_x4
+E2M1 = mybir.dt.float4_e2m1fn_x4
+ACT = mybir.ActivationFunctionType
+ALU = mybir.AluOpType
+
+P = 128
+PACK = 4
+QUADS = 4
+HALF = O // 2
+
+
+def tile_list_boardtwiceweighed_solo_further_weighedout_kernel(
+    tc, xt_words, xt_scales, w_words, w_scales, sa, sb, wb_words, wb_scales, ws_words, ws_scales, so,
+    offs, offs2, offs3, offs4, offs5, offs6, offs7, out,
+):
+    nc = tc.nc
+    with ExitStack() as ctx:
+        lists = ctx.enter_context(tc.tile_pool(name="lists", bufs=1))
+        sb_pool = ctx.enter_context(tc.tile_pool(name="work", bufs=1))
+        psum = ctx.enter_context(tc.psum_pool(name="psum", bufs=1))
+
+        def tile(name, cols, dtype):
+            return sb_pool.tile([P] + cols, dtype, name=name, align_bytes=64)
+
+        def load_list(name, source):
+            held = lists.tile(list(source.shape), U16, name=name)
+            nc.sync.dma_start(held[:], source)
+            return held
+
+        def load_plane(queue, plane, rows):
+            for q in range(QUADS):
+                queue.dma_start(plane[32 * q : 32 * q + 4, :].bitcast(I32), rows[0, 4 * q : 4 * q + 4, :].bitcast(I32))
+
+        xt_plane = tile("xt_plane", [T], U8)
+        w_plane = tile("w_plane", [R], U8)
+        wb_plane = tile("wb_plane", [N], U8)
+        ws_plane = tile("ws_plane", [N], U8)
+        boards = [tile(f"board{t}", [C], F32) for t in range(PACK)]
+        nc.vector.memset(xt_plane[:].bitcast(I32), 0)
+        nc.vector.memset(w_plane[:].bitcast(I32), 0)
+
+        l1 = load_list("l1", offs)
+        w_rows = sb_pool.tile([4, QUADS, R // 4], I32, name="w_rows", align_bytes=64)
+        nc.sync.dma_start(w_rows[:], w_scales[0].bitcast(I32).rearrange("(q r) c -> r q c", r=4))
+        xt_codes = tile("xt_codes", [T], U32)
+        nc.sync.dma_start(xt_codes[:].bitcast(I32), xt_words[0].rearrange("p n t -> p (n t)").bitcast(I32))
+        w_raw = tile("w_raw", [R], U16)
+        nc.sync.dma_start(w_raw[:].bitcast(I32), w_words[0].bitcast(I32))
+        load_plane(nc.scalar, xt_plane, xt_scales)
+
+        for board in boards:
+            nc.vector.memset(board[:], 0.0)
+        nc.vector.memset(wb_plane[:].bitcast(I32), 0)
+        nc.vector.memset(ws_plane[:].bitcast(I32), 0)
+
+        l5 = load_list("l5", offs5)
+        l2 = load_list("l2", offs2)
+        l3 = load_list("l3", offs3)
+        l4 = load_list("l4", offs4)
+        sa_cols = tile("sa_cols", [PACK], F32)
+        sb_cols = tile("sb_cols", [PACK], F32)
+        nc.sync.dma_start(sa_cols[:], sa.rearrange("(p t) one -> p (t one)", t=PACK))
+        nc.sync.dma_start(sb_cols[:], sb.rearrange("(p t) one -> p (t one)", t=PACK))
+        ws_codes = tile("ws_codes", [N], U16)
+        wb_codes = tile("wb_codes", [N], U16)
+        nc.sync.dma_start(ws_codes[:].bitcast(I32), ws_words[0].bitcast(I32))
+        nc.sync.dma_start(wb_codes[:].bitcast(I32), wb_words[0].bitcast(I32))
+        load_plane(nc.sync, ws_plane, ws_scales)
+        load_plane(nc.sync, wb_plane, wb_scales)
+        so_cols = [tile(f"so_col{h}", [1], F32) for h in range(2)]
+        for h in range(2):
+            nc.sync.dma_start(so_cols[h][:], so[h * P : (h + 1) * P, :])
+        l6 = load_list("l6", offs6)
+        l7 = load_list("l7", offs7)
+
+        for q in range(QUADS):
+            nc.vector.tensor_copy(w_plane[32 * q : 32 * q + 4, :].bitcast(I32), w_rows[:, q, :])
+        w_codes = tile("w_codes", [R], U16)
+        nc.scalar.copy(w_codes[:].rearrange("p (t m) -> p t m", t=PACK), w_raw[:].rearrange("p (m t) -> p t m", t=PACK))
+        x1_plane = tile("x1_plane", [J], U8)
+        nc.vector.tensor_copy(x1_plane[:], xt_plane[:].indirect(l1[:]))
+        w_dealt = tile("w_dealt", [R], U8)
+        nc.vector.tensor_copy(w_dealt[:].rearrange("p (t m) -> p t m", t=PACK), w_plane[:].rearrange("p (m t) -> p t m", t=PACK))
+        x1_codes = tile("x1_codes", [J], U32)
+        nc.vector.tensor_copy(x1_codes[:], xt_codes[:].indirect(l1[:]))
+
+        a_banks = [psum.tile([P, J], F32, name=f"a_bank{t}") for t in range(PACK)]
+        for t in range(PACK):
+            cols = slice(t * P, (t + 1) * P)
+            nc.tensor.matmul_mx(
+                out=a_banks[t][:], lhsT=w_codes[:, cols].bitcast(E2M1), lhsT_scale=w_dealt[:, cols],
+                rhs=x1_codes[:].bitcast(E5M2), rhs_scale=x1_plane[:], start=True, stop=True,
+            )
+
+        x5_codes = tile("x5_codes", [O], U32)
+        nc.vector.tensor_copy(x5_codes[:], xt_codes[:].indirect(l5[:]))
+
+        a_rows = [tile(f"a_rows{t}", [J], F32) for t in range(PACK)]
+        first = [tile(f"first{t}", [O], F32) for t in range(PACK)]
+        second = [tile(f"second{t}", [O], F32) for t in range(PACK)]
+        diff = tile("diff", [PACK, O], F32)
+
+        def fetch(t):
+            nc.scalar.activation(first[t][:], boards[t][:].indirect(l3[:]), ACT.Copy, scale=sa_cols[:, t : t + 1])
+            nc.scalar.activation(second[t][:], boards[t][:].indirect(l4[:]), ACT.Copy, scale=sb_cols[:, t : t + 1])
+
+        def subtract(t):
+            nc.vector.tensor_tensor(diff[:, t, :], first[t][:], second[t][:], ALU.subtract)
+
+        nc.vector.tensor_copy(a_rows[0][:], a_banks[0][:])
+        nc.scalar.activation(a_rows[1][:], a_banks[1][:], ACT.Copy)
+        nc.vector.tensor_copy(a_rows[2][:], a_banks[2][:])
+        nc.vector.tensor_copy(boards[0][:].indirect(l2[:]), a_rows[0][:])
+        nc.scalar.activation(boards[1][:].indirect(l2[:]), a_rows[1][:], ACT.Copy)
+        nc.vector.tensor_copy(a_rows[3][:], a_banks[3][:])
+        nc.vector.tensor_copy(boards[2][:].indirect(l2[:]), a_rows[2][:])
+        fetch(0)
+        nc.vector.tensor_copy(boards[3][:].indirect(l2[:]), a_rows[3][:])
+        fetch(1)
+        x5_plane = tile("x5_plane", [O], U8)
+        nc.vector.tensor_copy(x5_plane[:], xt_plane[:].indirect(l5[:]))
+        fetch(2)
+        fetch(3)
+        for t in range(PACK):
+            subtract(t)
+
+        p_banks = [psum.tile([P, O], F32, name=f"p_bank{h}") for h in range(2)]
+        for h in range(2):
+            cols = slice(h * P, (h + 1) * P)
+            nc.tensor.matmul_mx(
+                out=p_banks[h][:], lhsT=ws_codes[:, cols].bitcast(E2M1), lhsT_scale=ws_plane[:, cols],
+                rhs=x5_codes[:].bitcast(E5M2), rhs_scale=x5_plane[:], start=True, stop=False,
+            )
+
+        for g in range(2):
+            places = slice(g * HALF, (g + 1) * HALF)
+            hid = tile(f"hid{g}", [HALF, PACK], BF16)
+            nc.scalar.activation(hid[:], diff[:, :, places].rearrange("p t o -> p o t"), ACT.Abs)
+            hid_codes = tile(f"hid_codes{g}", [HALF], U32)
+            hid_plane = tile(f"hid_plane{g}", [HALF], U8)
+            nc.vector.quantize_mx(out=hid_codes[:].bitcast(E4M3), scales=hid_plane[:], in_=hid[:].rearrange("p o t -> p (o t)"))
+            for h in range(2):
+                cols = slice(h * P, (h + 1) * P)
+                nc.tensor.matmul_mx(
+                    out=p_banks[h][:, places], lhsT=wb_codes[:, cols].bitcast(E2M1), lhsT_scale=wb_plane[:, cols],
+                    rhs=hid_codes[:].bitcast(E4M3), rhs_scale=hid_plane[:], start=False, stop=(g == 1),
+                )
+
+        p_rows = [tile(f"p_rows{h}", [O], F32) for h in range(2)]
+        nc.scalar.activation(p_rows[0][:], p_banks[0][:], ACT.Copy)
+        nc.vector.tensor_copy(p_rows[1][:], p_banks[1][:])
+        for h in range(2):
+            weighed = tile(f"weighed{h}", [U], F32)
+            nc.scalar.activation(weighed[:], p_rows[h][:].indirect(l7[:]), ACT.Copy, scale=so_cols[h][:])
+            ends = tile(f"ends{h}", [U], F32)
+            nc.vector.tensor_tensor(ends[:], p_rows[h][:].indirect(l6[:]), weighed[:], ALU.subtract)
+            nc.sync.dma_start(out[h * P : (h + 1) * P, :], ends[:])

@@ -33,8 +33,8 @@ def tile_list_boardtwiceweighed_solo_further_weighedout_kernel(
         sb_pool = ctx.enter_context(tc.tile_pool(name="work", bufs=1))
         psum = ctx.enter_context(tc.psum_pool(name="psum", bufs=1))
 
-        def tile(name, cols, dtype):
-            return sb_pool.tile([P] + cols, dtype, name=name, align_bytes=64)
+        def tile(name, cols, dtype, tag=None):
+            return sb_pool.tile([P] + cols, dtype, name=name, tag=tag or name, align_bytes=64)
 
         def load_list(name, source):
             held = lists.tile(list(source.shape), U16, name=name)
@@ -64,8 +64,8 @@ def tile_list_boardtwiceweighed_solo_further_weighedout_kernel(
 
         for board in boards:
             nc.vector.memset(board[:], 0.0)
-        nc.vector.memset(wb_plane[:].bitcast(I32), 0)
-        nc.vector.memset(ws_plane[:].bitcast(I32), 0)
+        nc.gpsimd.memset(wb_plane[:].bitcast(I32), 0)
+        nc.gpsimd.memset(ws_plane[:].bitcast(I32), 0)
 
         l5 = load_list("l5", offs5)
         l2 = load_list("l2", offs2)
@@ -108,64 +108,73 @@ def tile_list_boardtwiceweighed_solo_further_weighedout_kernel(
 
         x5_codes = tile("x5_codes", [O], U32)
         nc.vector.tensor_copy(x5_codes[:], xt_codes[:].indirect(l5[:]))
-
-        a_rows = [tile(f"a_rows{t}", [J], F32) for t in range(PACK)]
-        first = [tile(f"first{t}", [O], F32) for t in range(PACK)]
-        second = [tile(f"second{t}", [O], F32) for t in range(PACK)]
-        diff = tile("diff", [PACK, O], F32)
-
-        def fetch(t):
-            nc.scalar.activation(first[t][:], boards[t][:].indirect(l3[:]), ACT.Copy, scale=sa_cols[:, t : t + 1])
-            nc.scalar.activation(second[t][:], boards[t][:].indirect(l4[:]), ACT.Copy, scale=sb_cols[:, t : t + 1])
-
-        def subtract(t):
-            nc.vector.tensor_tensor(diff[:, t, :], first[t][:], second[t][:], ALU.subtract)
-
-        nc.vector.tensor_copy(a_rows[0][:], a_banks[0][:])
-        nc.scalar.activation(a_rows[1][:], a_banks[1][:], ACT.Copy)
-        nc.vector.tensor_copy(a_rows[2][:], a_banks[2][:])
-        nc.vector.tensor_copy(boards[0][:].indirect(l2[:]), a_rows[0][:])
-        nc.scalar.activation(boards[1][:].indirect(l2[:]), a_rows[1][:], ACT.Copy)
-        nc.vector.tensor_copy(a_rows[3][:], a_banks[3][:])
-        nc.vector.tensor_copy(boards[2][:].indirect(l2[:]), a_rows[2][:])
-        fetch(0)
-        nc.vector.tensor_copy(boards[3][:].indirect(l2[:]), a_rows[3][:])
-        fetch(1)
         x5_plane = tile("x5_plane", [O], U8)
         nc.vector.tensor_copy(x5_plane[:], xt_plane[:].indirect(l5[:]))
-        fetch(2)
-        fetch(3)
-        for t in range(PACK):
-            subtract(t)
 
-        p_banks = [psum.tile([P, O], F32, name=f"p_bank{h}") for h in range(2)]
-        for h in range(2):
-            cols = slice(h * P, (h + 1) * P)
-            nc.tensor.matmul_mx(
-                out=p_banks[h][:], lhsT=ws_codes[:, cols].bitcast(E2M1), lhsT_scale=ws_plane[:, cols],
-                rhs=x5_codes[:].bitcast(E5M2), rhs_scale=x5_plane[:], start=True, stop=False,
-            )
+        a_rows = [tile(f"a_rows{t}", [J], F32) for t in range(PACK)]
+        first = tile("first", [PACK - 1, O], F32)
+        second = tile("second", [PACK - 1, O], F32)
+        first_last = [tile(f"first_last{g}", [HALF], F32) for g in range(2)]
+        second_last = [tile(f"second_last{g}", [HALF], F32) for g in range(2)]
+        diff = tile("diff", [PACK, O], F32)
+        whole = slice(0, O)
+        halves = [slice(g * HALF, (g + 1) * HALF) for g in range(2)]
 
-        for g in range(2):
-            places = slice(g * HALF, (g + 1) * HALF)
+        def fetch(t, places, into_first, into_second):
+            entries = slice(places.start // 16, places.stop // 16)
+            nc.scalar.activation(into_first, boards[t][:].indirect(l3[:, entries]), ACT.Copy, scale=sa_cols[:, t : t + 1])
+            nc.scalar.activation(into_second, boards[t][:].indirect(l4[:, entries]), ACT.Copy, scale=sb_cols[:, t : t + 1])
+
+        nc.scalar.activation(a_rows[0][:], a_banks[0][:], ACT.Copy)
+        nc.scalar.activation(a_rows[1][:], a_banks[1][:], ACT.Copy)
+        nc.vector.tensor_copy(a_rows[2][:], a_banks[2][:])
+        nc.scalar.activation(boards[0][:].indirect(l2[:]), a_rows[0][:], ACT.Copy)
+        nc.vector.tensor_copy(boards[1][:].indirect(l2[:]), a_rows[1][:])
+        nc.vector.tensor_copy(a_rows[3][:], a_banks[3][:])
+        nc.vector.tensor_copy(boards[2][:].indirect(l2[:]), a_rows[2][:])
+        nc.vector.tensor_copy(boards[3][:].indirect(l2[:]), a_rows[3][:])
+        for t in range(PACK - 1):
+            fetch(t, whole, first[:, t, :], second[:, t, :])
+        nc.vector.tensor_tensor(diff[:, 0:3, :], first[:], second[:], ALU.subtract)
+        for g, places in enumerate(halves):
+            fetch(3, places, first_last[g][:], second_last[g][:])
+        nc.vector.tensor_tensor(diff[:, 3, halves[0]], first_last[0][:], second_last[0][:], ALU.subtract)
+        nc.vector.tensor_tensor(diff[:, 3, halves[1]], first_last[1][:], second_last[1][:], ALU.subtract)
+
+        p_banks = [[psum.tile([P, HALF], F32, name=f"p_bank{g}{h}") for h in range(2)] for g in range(2)]
+        p_rows = [tile(f"p_rows{h}", [O], F32) for h in range(2)]
+        for g, places in enumerate(halves):
+            for h in range(2):
+                cols = slice(h * P, (h + 1) * P)
+                nc.tensor.matmul_mx(
+                    out=p_banks[g][h][:], lhsT=ws_codes[:, cols].bitcast(E2M1), lhsT_scale=ws_plane[:, cols],
+                    rhs=x5_codes[:, places].bitcast(E5M2), rhs_scale=x5_plane[:, places], start=True, stop=False,
+                )
+
+        for g, places in enumerate(halves):
             hid = tile(f"hid{g}", [HALF, PACK], BF16)
-            nc.scalar.activation(hid[:], diff[:, :, places].rearrange("p t o -> p o t"), ACT.Abs)
+            nc.scalar.activation(
+                hid[:].rearrange("p (c i) t -> p c t i", i=4), diff[:, :, places].rearrange("p t (c i) -> p c t i", i=4), ACT.Abs
+            )
             hid_codes = tile(f"hid_codes{g}", [HALF], U32)
             hid_plane = tile(f"hid_plane{g}", [HALF], U8)
             nc.vector.quantize_mx(out=hid_codes[:].bitcast(E4M3), scales=hid_plane[:], in_=hid[:].rearrange("p o t -> p (o t)"))
             for h in range(2):
                 cols = slice(h * P, (h + 1) * P)
                 nc.tensor.matmul_mx(
-                    out=p_banks[h][:, places], lhsT=wb_codes[:, cols].bitcast(E2M1), lhsT_scale=wb_plane[:, cols],
-                    rhs=hid_codes[:].bitcast(E4M3), rhs_scale=hid_plane[:], start=False, stop=(g == 1),
+                    out=p_banks[g][h][:], lhsT=wb_codes[:, cols].bitcast(E2M1), lhsT_scale=wb_plane[:, cols],
+                    rhs=hid_codes[:].bitcast(E4M3), rhs_scale=hid_plane[:], start=False, stop=True,
                 )
+        for g, places in enumerate(halves):
+            for h in range(2):
+                nc.vector.tensor_copy(p_rows[h][:, places], p_banks[g][h][:])
 
-        p_rows = [tile(f"p_rows{h}", [O], F32) for h in range(2)]
-        nc.scalar.activation(p_rows[0][:], p_banks[0][:], ACT.Copy)
-        nc.vector.tensor_copy(p_rows[1][:], p_banks[1][:])
+        weighed = [tile(f"weighed{h}", [U], F32) for h in range(2)]
+        picked = [tile(f"picked{h}", [U], F32) for h in range(2)]
         for h in range(2):
-            weighed = tile(f"weighed{h}", [U], F32)
-            nc.scalar.activation(weighed[:], p_rows[h][:].indirect(l7[:]), ACT.Copy, scale=so_cols[h][:])
+            nc.scalar.activation(weighed[h][:], p_rows[h][:].indirect(l7[:]), ACT.Copy, scale=so_cols[h][:])
+            nc.vector.tensor_copy(picked[h][:], p_rows[h][:].indirect(l6[:]))
+        for h in range(2):
             ends = tile(f"ends{h}", [U], F32)
-            nc.vector.tensor_tensor(ends[:], p_rows[h][:].indirect(l6[:]), weighed[:], ALU.subtract)
+            nc.vector.tensor_tensor(ends[:], picked[h][:], weighed[h][:], ALU.subtract)
             nc.sync.dma_start(out[h * P : (h + 1) * P, :], ends[:])

@@ -68,12 +68,12 @@ def tile_list_boardtwiceweighed_solo_further_weighedout_kernel(
         nc.gpsimd.memset(ws_plane[:].bitcast(I32), 0)
 
         l5 = load_list("l5", offs5)
-        l2 = load_list("l2", offs2)
         l3 = load_list("l3", offs3)
         l4 = load_list("l4", offs4)
         sa_cols = tile("sa_cols", [PACK], F32)
         sb_cols = tile("sb_cols", [PACK], F32)
         nc.sync.dma_start(sa_cols[:], sa.rearrange("(p t) one -> p (t one)", t=PACK))
+        l2 = load_list("l2", offs2)
         nc.sync.dma_start(sb_cols[:], sb.rearrange("(p t) one -> p (t one)", t=PACK))
         ws_codes = tile("ws_codes", [N], U16)
         wb_codes = tile("wb_codes", [N], U16)
@@ -93,16 +93,18 @@ def tile_list_boardtwiceweighed_solo_further_weighedout_kernel(
         nc.scalar.copy(w_codes[:].rearrange("p (t m) -> p t m", t=PACK), w_raw[:].rearrange("p (m t) -> p t m", t=PACK))
         x1_plane = tile("x1_plane", [J], U8)
         nc.vector.tensor_copy(x1_plane[:], xt_plane[:].indirect(l1[:]))
-        w_dealt = tile("w_dealt", [R], U8)
-        nc.vector.tensor_copy(w_dealt[:].rearrange("p (t m) -> p t m", t=PACK), w_plane[:].rearrange("p (m t) -> p t m", t=PACK))
+        w_dealt = [tile(f"w_dealt{u}", [2, P], U8) for u in range(2)]
+        w_scale_cols = w_plane[:].rearrange("p (m t) -> p t m", t=PACK)
+        nc.vector.tensor_copy(w_dealt[0][:], w_scale_cols[:, 0:2, :])
         x1_codes = tile("x1_codes", [J], U32)
         nc.vector.tensor_copy(x1_codes[:], xt_codes[:].indirect(l1[:]))
+        nc.vector.tensor_copy(w_dealt[1][:], w_scale_cols[:, 2:4, :])
 
         a_banks = [psum.tile([P, J], F32, name=f"a_bank{t}") for t in range(PACK)]
         for t in range(PACK):
             cols = slice(t * P, (t + 1) * P)
             nc.tensor.matmul_mx(
-                out=a_banks[t][:], lhsT=w_codes[:, cols].bitcast(E2M1), lhsT_scale=w_dealt[:, cols],
+                out=a_banks[t][:], lhsT=w_codes[:, cols].bitcast(E2M1), lhsT_scale=w_dealt[t // 2][:, t % 2, :],
                 rhs=x1_codes[:].bitcast(E5M2), rhs_scale=x1_plane[:], start=True, stop=True,
             )
 
@@ -153,8 +155,13 @@ def tile_list_boardtwiceweighed_solo_further_weighedout_kernel(
 
         for g, places in enumerate(halves):
             hid = tile(f"hid{g}", [HALF, PACK], BF16)
+            on_vector = HALF // 2 if g == 0 else 0
+            if on_vector:
+                woven = diff[:, :, 0:on_vector].rearrange("p t o -> p o t")
+                nc.vector.scalar_tensor_tensor(hid[:, 0:on_vector, :], woven, -1.0, woven, ALU.mult, ALU.max)
             nc.scalar.activation(
-                hid[:].rearrange("p (c i) t -> p c t i", i=4), diff[:, :, places].rearrange("p t (c i) -> p c t i", i=4), ACT.Abs
+                hid[:, on_vector:, :].rearrange("p (c i) t -> p c t i", i=4),
+                diff[:, :, places.start + on_vector : places.stop].rearrange("p t (c i) -> p c t i", i=4), ACT.Abs,
             )
             hid_codes = tile(f"hid_codes{g}", [HALF], U32)
             hid_plane = tile(f"hid_plane{g}", [HALF], U8)

@@ -68,12 +68,12 @@ def tile_list_boardtwiceweighed_solo_further_weighedout_kernel(
         nc.gpsimd.memset(ws_plane[:].bitcast(I32), 0)
 
         l5 = load_list("l5", offs5)
+        l2 = load_list("l2", offs2)
         l3 = load_list("l3", offs3)
         l4 = load_list("l4", offs4)
         sa_cols = tile("sa_cols", [PACK], F32)
         sb_cols = tile("sb_cols", [PACK], F32)
         nc.sync.dma_start(sa_cols[:], sa.rearrange("(p t) one -> p (t one)", t=PACK))
-        l2 = load_list("l2", offs2)
         nc.sync.dma_start(sb_cols[:], sb.rearrange("(p t) one -> p (t one)", t=PACK))
         ws_codes = tile("ws_codes", [N], U16)
         wb_codes = tile("wb_codes", [N], U16)
@@ -155,13 +155,8 @@ def tile_list_boardtwiceweighed_solo_further_weighedout_kernel(
 
         for g, places in enumerate(halves):
             hid = tile(f"hid{g}", [HALF, PACK], BF16)
-            on_vector = HALF // 2 if g == 0 else 0
-            if on_vector:
-                woven = diff[:, :, 0:on_vector].rearrange("p t o -> p o t")
-                nc.vector.scalar_tensor_tensor(hid[:, 0:on_vector, :], woven, -1.0, woven, ALU.mult, ALU.max)
             nc.scalar.activation(
-                hid[:, on_vector:, :].rearrange("p (c i) t -> p c t i", i=4),
-                diff[:, :, places.start + on_vector : places.stop].rearrange("p t (c i) -> p c t i", i=4), ACT.Abs,
+                hid[:].rearrange("p (c i) t -> p c t i", i=4), diff[:, :, places].rearrange("p t (c i) -> p c t i", i=4), ACT.Abs
             )
             hid_codes = tile(f"hid_codes{g}", [HALF], U32)
             hid_plane = tile(f"hid_plane{g}", [HALF], U8)
@@ -172,9 +167,10 @@ def tile_list_boardtwiceweighed_solo_further_weighedout_kernel(
                     out=p_banks[g][h][:], lhsT=wb_codes[:, cols].bitcast(E2M1), lhsT_scale=wb_plane[:, cols],
                     rhs=hid_codes[:].bitcast(E4M3), rhs_scale=hid_plane[:], start=False, stop=True,
                 )
-        for g, places in enumerate(halves):
-            for h in range(2):
-                nc.vector.tensor_copy(p_rows[h][:, places], p_banks[g][h][:])
+        for h in range(2):
+            nc.vector.tensor_copy(p_rows[h][:, halves[0]], p_banks[0][h][:])
+        nc.vector.tensor_copy(p_rows[0][:, halves[1]], p_banks[1][0][:])
+        nc.scalar.activation(p_rows[1][:, halves[1]], p_banks[1][1][:], ACT.Copy)
 
         weighed = [tile(f"weighed{h}", [U], F32) for h in range(2)]
         picked = [tile(f"picked{h}", [U], F32) for h in range(2)]

from contextlib import ExitStack

import concourse.mybir as mybir

K, T, J, R, C, O, N, U = 512, 1024, 256, 512, 512, 256, 256, 128
FLOPS = 2 * K * R * J + 2 * R * N * O + 2 * K * N * O

F32 = mybir.dt.float32
BF16 = mybir.dt.bfloat16
I32 = mybir.dt.int32
U32 = mybir.dt.uint32
U16 = mybir.dt.uint16
U8 = mybir.dt.uint8
E4M3 = mybir.dt.float8_e4m3fn_x4
E5M2 = mybir.dt.float8_e5m2_x4
E2M1 = mybir.dt.float4_e2m1fn_x4
ACT = mybir.ActivationFunctionType
ALU = mybir.AluOpType

P = 128
PACK = 4
QUADS = 4
HALF = O // 2


def tile_list_boardtwiceweighed_solo_further_weighedout_kernel(
    tc, xt_words, xt_scales, w_words, w_scales, sa, sb, wb_words, wb_scales, ws_words, ws_scales, so,
    offs, offs2, offs3, offs4, offs5, offs6, offs7, out,
):
    nc = tc.nc
    with ExitStack() as ctx:
        lists = ctx.enter_context(tc.tile_pool(name="lists", bufs=1))
        sb_pool = ctx.enter_context(tc.tile_pool(name="work", bufs=1))
        psum = ctx.enter_context(tc.psum_pool(name="psum", bufs=1))

        def tile(name, cols, dtype, tag=None):
            return sb_pool.tile([P] + cols, dtype, name=name, tag=tag or name, align_bytes=64)

        def load_list(name, source):
            held = lists.tile(list(source.shape), U16, name=name)
            nc.sync.dma_start(held[:], source)
            return held

        def load_plane(queue, plane, rows):
            for q in range(QUADS):
                queue.dma_start(plane[32 * q : 32 * q + 4, :].bitcast(I32), rows[0, 4 * q : 4 * q + 4, :].bitcast(I32))

        xt_plane = tile("xt_plane", [T], U8)
        w_plane = tile("w_plane", [R], U8)
        wb_plane = tile("wb_plane", [N], U8)
        ws_plane = tile("ws_plane", [N], U8)
        boards = [tile(f"board{t}", [C], F32) for t in range(PACK)]
        nc.vector.memset(xt_plane[:].bitcast(I32), 0)
        nc.vector.memset(w_plane[:].bitcast(I32), 0)

        l1 = load_list("l1", offs)
        w_rows = sb_pool.tile([4, QUADS, R // 4], I32, name="w_rows", align_bytes=64)
        nc.sync.dma_start(w_rows[:], w_scales[0].bitcast(I32).rearrange("(q r) c -> r q c", r=4))
        xt_codes = tile("xt_codes", [T], U32)
        nc.sync.dma_start(xt_codes[:].bitcast(I32), xt_words[0].rearrange("p n t -> p (n t)").bitcast(I32))
        w_raw = tile("w_raw", [R], U16)
        nc.sync.dma_start(w_raw[:].bitcast(I32), w_words[0].bitcast(I32))
        load_plane(nc.scalar, xt_plane, xt_scales)

        for board in boards:
            nc.vector.memset(board[:], 0.0)
        nc.gpsimd.memset(wb_plane[:].bitcast(I32), 0)
        nc.gpsimd.memset(ws_plane[:].bitcast(I32), 0)

        l5 = load_list("l5", offs5)
        l2 = load_list("l2", offs2)
        l3 = load_list("l3", offs3)
        l4 = load_list("l4", offs4)
        sa_cols = tile("sa_cols", [PACK], F32)
        sb_cols = tile("sb_cols", [PACK], F32)
        nc.sync.dma_start(sa_cols[:], sa.rearrange("(p t) one -> p (t one)", t=PACK))
        nc.sync.dma_start(sb_cols[:], sb.rearrange("(p t) one -> p (t one)", t=PACK))
        ws_codes = tile("ws_codes", [N], U16)
        wb_codes = tile("wb_codes", [N], U16)
        nc.sync.dma_start(ws_codes[:].bitcast(I32), ws_words[0].bitcast(I32))
        nc.sync.dma_start(wb_codes[:].bitcast(I32), wb_words[0].bitcast(I32))
        load_plane(nc.sync, ws_plane, ws_scales)
        load_plane(nc.sync, wb_plane, wb_scales)
        so_cols = [tile(f"so_col{h}", [1], F32) for h in range(2)]
        for h in range(2):
            nc.sync.dma_start(so_cols[h][:], so[h * P : (h + 1) * P, :])
        l6 = load_list("l6", offs6)
        l7 = load_list("l7", offs7)

        for q in range(QUADS):
            nc.vector.tensor_copy(w_plane[32 * q : 32 * q + 4, :].bitcast(I32), w_rows[:, q, :])
        w_codes = tile("w_codes", [R], U16)
        nc.scalar.copy(w_codes[:].rearrange("p (t m) -> p t m", t=PACK), w_raw[:].rearrange("p (m t) -> p t m", t=PACK))
        x1_plane = tile("x1_plane", [J], U8)
        nc.vector.tensor_copy(x1_plane[:], xt_plane[:].indirect(l1[:]))
        w_dealt = [tile(f"w_dealt{u}", [2, P], U8) for u in range(2)]
        w_scale_cols = w_plane[:].rearrange("p (m t) -> p t m", t=PACK)
        nc.vector.tensor_copy(w_dealt[0][:], w_scale_cols[:, 0:2, :])
        x1_codes = tile("x1_codes", [J], U32)
        nc.vector.tensor_copy(x1_codes[:], xt_codes[:].indirect(l1[:]))
        nc.vector.tensor_copy(w_dealt[1][:], w_scale_cols[:, 2:4, :])

        a_banks = [psum.tile([P, J], F32, name=f"a_bank{t}") for t in range(PACK)]
        for t in range(PACK):
            cols = slice(t * P, (t + 1) * P)
            nc.tensor.matmul_mx(
                out=a_banks[t][:], lhsT=w_codes[:, cols].bitcast(E2M1), lhsT_scale=w_dealt[t // 2][:, t % 2, :],
                rhs=x1_codes[:].bitcast(E5M2), rhs_scale=x1_plane[:], start=True, stop=True,
            )

        x5_codes = tile("x5_codes", [O], U32)
        nc.vector.tensor_copy(x5_codes[:], xt_codes[:].indirect(l5[:]))
        x5_plane = tile("x5_plane", [O], U8)
        nc.vector.tensor_copy(x5_plane[:], xt_plane[:].indirect(l5[:]))

        a_rows = [tile(f"a_rows{t}", [J], F32) for t in range(PACK)]
        first = tile("first", [PACK - 1, O], F32)
        second = tile("second", [PACK - 1, O], F32)
        first_last = [tile(f"first_last{g}", [HALF], F32) for g in range(2)]
        second_last = [tile(f"second_last{g}", [HALF], F32) for g in range(2)]
        diff = tile("diff", [PACK, O], F32)
        whole = slice(0, O)
        halves = [slice(g * HALF, (g + 1) * HALF) for g in range(2)]

        def fetch(t, places, into_first, into_second):
            entries = slice(places.start // 16, places.stop // 16)
            nc.scalar.activation(into_first, boards[t][:].indirect(l3[:, entries]), ACT.Copy, scale=sa_cols[:, t : t + 1])
            nc.scalar.activation(into_second, boards[t][:].indirect(l4[:, entries]), ACT.Copy, scale=sb_cols[:, t : t + 1])

        nc.scalar.activation(a_rows[0][:], a_banks[0][:], ACT.Copy)
        nc.scalar.activation(a_rows[1][:], a_banks[1][:], ACT.Copy)
        nc.vector.tensor_copy(a_rows[2][:], a_banks[2][:])
        nc.scalar.activation(boards[0][:].indirect(l2[:]), a_rows[0][:], ACT.Copy)
        nc.vector.tensor_copy(boards[1][:].indirect(l2[:]), a_rows[1][:])
        nc.vector.tensor_copy(a_rows[3][:], a_banks[3][:])
        nc.vector.tensor_copy(boards[2][:].indirect(l2[:]), a_rows[2][:])
        nc.vector.tensor_copy(boards[3][:].indirect(l2[:]), a_rows[3][:])
        for t in range(PACK - 1):
            fetch(t, whole, first[:, t, :], second[:, t, :])
        nc.vector.tensor_tensor(diff[:, 0:3, :], first[:], second[:], ALU.subtract)
        for g, places in enumerate(halves):
            fetch(3, places, first_last[g][:], second_last[g][:])
        nc.vector.tensor_tensor(diff[:, 3, halves[0]], first_last[0][:], second_last[0][:], ALU.subtract)
        nc.vector.tensor_tensor(diff[:, 3, halves[1]], first_last[1][:], second_last[1][:], ALU.subtract)

        p_banks = [[psum.tile([P, HALF], F32, name=f"p_bank{g}{h}") for h in range(2)] for g in range(2)]
        p_rows = [tile(f"p_rows{h}", [O], F32) for h in range(2)]
        for g, places in enumerate(halves):
            for h in range(2):
                cols = slice(h * P, (h + 1) * P)
                nc.tensor.matmul_mx(
                    out=p_banks[g][h][:], lhsT=ws_codes[:, cols].bitcast(E2M1), lhsT_scale=ws_plane[:, cols],
                    rhs=x5_codes[:, places].bitcast(E5M2), rhs_scale=x5_plane[:, places], start=True, stop=False,
                )

        for g, places in enumerate(halves):
            hid = tile(f"hid{g}", [HALF, PACK], BF16)
            nc.scalar.activation(
                hid[:].rearrange("p (c i) t -> p c t i", i=4), diff[:, :, places].rearrange("p t (c i) -> p c t i", i=4), ACT.Abs
            )
            hid_codes = tile(f"hid_codes{g}", [HALF], U32)
            hid_plane = tile(f"hid_plane{g}", [HALF], U8)
            nc.vector.quantize_mx(out=hid_codes[:].bitcast(E4M3), scales=hid_plane[:], in_=hid[:].rearrange("p o t -> p (o t)"))
            for h in range(2):
                cols = slice(h * P, (h + 1) * P)
                nc.tensor.matmul_mx(
                    out=p_banks[g][h][:], lhsT=wb_codes[:, cols].bitcast(E2M1), lhsT_scale=wb_plane[:, cols],
                    rhs=hid_codes[:].bitcast(E4M3), rhs_scale=hid_plane[:], start=False, stop=True,
                )
        for h in range(2):
            nc.vector.tensor_copy(p_rows[h][:, halves[0]], p_banks[0][h][:])
        nc.vector.tensor_copy(p_rows[0][:, halves[1]], p_banks[1][0][:])
        nc.scalar.activation(p_rows[1][:, halves[1]], p_banks[1][1][:], ACT.Copy)

        weighed = [tile(f"weighed{h}", [U], F32) for h in range(2)]
        picked = [tile(f"picked{h}", [U], F32) for h in range(2)]
        for h in range(2):
            nc.scalar.activation(weighed[h][:], p_rows[h][:].indirect(l7[:]), ACT.Copy, scale=so_cols[h][:])
            nc.vector.tensor_copy(picked[h][:], p_rows[h][:].indirect(l6[:]))
        for h in range(2):
            ends = tile(f"ends{h}", [U], F32)
            nc.vector.tensor_tensor(ends[:], picked[h][:], weighed[h][:], ALU.subtract)
            nc.sync.dma_start(out[h * P : (h + 1) * P, :], ends[:])
